import numpy as np
import ml_dtypes


def mxq(x, axis, fmt="e4m3"):
    dtype, down = {"e4m3": (ml_dtypes.float8_e4m3fn, 7), "e5m2": (ml_dtypes.float8_e5m2, 14)}[fmt]
    v = np.moveaxis(np.asarray(x, np.float32).astype(ml_dtypes.bfloat16).astype(np.float64), axis, -1)
    blocks = v.reshape(v.shape[:-1] + (-1, 32))
    amax = np.abs(blocks).max(-1, keepdims=True)
    byte = np.maximum(np.where(amax > 0, np.frexp(amax)[1] - 1 + 127, 0) - down, 1)
    scale = np.exp2(byte - 127.0)
    codes = (blocks / scale).astype(np.float32).astype(dtype).astype(np.float64)
    return np.moveaxis((codes * scale).reshape(v.shape), -1, axis)


WIDE = False


def mx_kscale(k):
    if not WIDE:
        return np.ones(k)
    levels = np.array([10, -10, 5, -5, 0])
    if k % 512:
        return np.exp2(np.random.permutation(np.resize(levels, k // 32))).repeat(32)
    a = np.empty((k // 512, 16))
    for p in range(k // 512):
        a[p, :8] = np.random.permutation(np.resize(levels, 8))
        for g in range(8):
            far = levels[np.abs(levels - a[p, g]) >= 10]
            a[p, g + 8] = far[np.random.randint(len(far))]
    return np.exp2(a.ravel()).repeat(32)


def f64(x):
    return np.asarray(x).astype(np.float64)


def striped(idx):
    return np.tile(idx.reshape(-1, 16).T, (8, 1)).astype(np.uint16)


def unstriped(offs):
    return offs[:16].T.reshape(-1).astype(np.int64)


E2M1 = np.array([0.0, 0.5, 1.0, 1.5, 2.0, 3.0, 4.0, 6.0, -0.0, -0.5, -1.0, -1.5, -2.0, -3.0, -4.0, -6.0])


def pack_weight(w, fmt):
    k, n = w.shape
    w = f64(np.asarray(w, np.float32).astype(ml_dtypes.bfloat16)).reshape(k // 32, 32, n)
    amax = np.abs(w).max(1)
    if fmt == "e4m3":
        byte = np.frexp(amax)[1] - 1 + 127 - 7
    else:
        mant, ex = np.frexp(amax / 6.0)
        byte = np.where(mant > 0.5, ex, ex - 1) + 127
    byte = np.clip(np.where(amax > 0, byte, 1), 1, 254)
    scaled = (w * np.exp2(127.0 - byte)[:, None, :]).reshape(k, n).astype(np.float32)
    by_word = np.ascontiguousarray(scaled.reshape(k // 512, 128, 4, n).transpose(0, 1, 3, 2))
    if fmt == "e4m3":
        words = by_word.astype(ml_dtypes.float8_e4m3fn).view(np.uint8)
    else:
        c = by_word.astype(ml_dtypes.float4_e2m1fn).view(np.uint8) & 0xF
        words = (c[..., 0::2] | (c[..., 1::2] << 4)).reshape(k // 512, 128, 2 * n)
    return np.ascontiguousarray(words), np.ascontiguousarray(byte.astype(np.uint8).reshape(k // 512, 16, n))


def unpack_weight(words, scales, fmt):
    g, _, n = scales.shape
    words = np.ascontiguousarray(words).reshape(g, 128, n, -1)
    if fmt == "e4m3":
        vals = words.view(ml_dtypes.float8_e4m3fn).astype(np.float64)
    else:
        nib = np.empty((g, 128, n, 4), np.uint8)
        nib[..., 0::2] = words & 0xF
        nib[..., 1::2] = words >> 4
        vals = E2M1[nib]
    vals = vals * np.repeat(np.exp2(scales.astype(np.float64) - 127.0), 8, axis=1)[..., None]
    return vals.transpose(0, 1, 3, 2).reshape(g * 512, n)


def gelu(v):
    return 0.5 * v * (1.0 + np.tanh(np.sqrt(2.0 / np.pi) * (v + 0.044715 * v**3)))


def striped8(idx):
    return np.concatenate([v.reshape(-1, 16).T for v in idx]).astype(np.uint16)


def unstriped8(offs):
    return np.stack([offs[16 * g:16 * g + 16].T.reshape(-1) for g in range(8)]).astype(np.int64)


def runs(v, idx8):
    k = np.arange(v.shape[0])
    return v[k[:, None], idx8[k % 512 // 64]]


K, T, S, P, H, N = 512, 2048, 1024, 512, 1024, 512

def setup_inputs():
    n = np.random.standard_normal
    s = mx_kscale(K)[:, None]
    u = mx_kscale(H)[:, None]
    d = {}
    d["tab_words"], d["tab_scales"] = pack_weight(n((K, T)) * s, "e4m3")
    d["offs"] = striped8(np.stack([np.random.permutation(T)[:S] for _ in range(8)]))
    d["pos1"] = striped(np.random.permutation(S)[:P])
    d["pos2"] = striped(np.random.permutation(S)[:P])
    d["w1"] = (n((K, H)) / s / K ** 0.5).astype(np.float32)
    d["w2_words"], d["w2_scales"] = pack_weight(n((K, H)) / s / K ** 0.5, "e2m1")
    d["w3"] = (n((K, H)) / s * u.T / K ** 0.5).astype(np.float32)
    d["w4_words"], d["w4_scales"] = pack_weight(n((H, N)) / u / H ** 0.5, "e4m3")
    return d

def reference(tab_words, tab_scales, offs, pos1, pos2, w1, w2_words, w2_scales, w3, w4_words, w4_scales):
    v = runs(unpack_weight(tab_words, tab_scales, "e4m3"), unstriped8(offs))
    a = mxq(f64(w1), 0, "e4m3").T @ v
    b = unpack_weight(w2_words, w2_scales, "e2m1").T @ v
    c = mxq(f64(w3), 0, "e4m3").T @ v
    h = np.maximum(a, b) * c
    lead = h[:, unstriped(pos1)]
    trail = h[:, unstriped(pos2)]
    z = np.abs(lead) + trail
    y = unpack_weight(w4_words, w4_scales, "e4m3").T @ mxq(z, 0, "e4m3")
    return np.log(1.0 + np.square(y))

@@ -1,0 +1,273 @@
+from contextlib import ExitStack
+
+import concourse.mybir as mybir
+
+K, T, S, PK, H, N = 512, 2048, 1024, 512, 1024, 512
+FLOPS = 2 * (3 * K * H * S + H * N * PK)
+
+F32 = mybir.dt.float32
+BF16 = mybir.dt.bfloat16
+I32 = mybir.dt.int32
+U32 = mybir.dt.uint32
+U16 = mybir.dt.uint16
+U8 = mybir.dt.uint8
+FP8X4 = mybir.dt.float8_e4m3fn_x4
+FP4X4 = mybir.dt.float4_e2m1fn_x4
+ALU = mybir.AluOpType
+ACT = mybir.ActivationFunctionType
+
+P = 128
+BANK = 512
+HALF = 256
+
+
+def tile_list_belt_ejector_strengths_kernel(
+    tc, tab_words, tab_scales, offs, pos1, pos2, w1, w2_words, w2_scales, w3, w4_words, w4_scales, out
+):
+    nc = tc.nc
+    with ExitStack() as ctx:
+        lists = ctx.enter_context(tc.tile_pool(name="lists", bufs=1))
+        keep = ctx.enter_context(tc.tile_pool(name="keep", bufs=1))
+        ring = ctx.enter_context(tc.tile_pool(name="ring", bufs=4))
+        psum = ctx.enter_context(tc.psum_pool(name="psum", bufs=1))
+
+        offs_t = lists.tile([P, S // 16], U16, name="offs_t")
+        pos1_t = lists.tile([P, PK // 16], U16, name="pos1_t")
+        pos2_t = lists.tile([P, PK // 16], U16, name="pos2_t")
+
+        w2s_raw = keep.tile([P, H], U8, name="w2s_raw", align_bytes=64)
+        tabs = keep.tile([P, T], U8, name="tabs", tag="tabs", align_bytes=64)
+
+        warm = keep.tile([P, 8], F32, name="warm")
+        nc.gpsimd.memset(warm[:], 1.0)
+        nc.scalar.activation(warm[:, 0:1], warm[:, 4:5], ACT.Ln)
+
+        nc.sync.dma_start(offs_t[:], offs)
+        nc.sync.dma_start(
+            out=tabs[:].bitcast(I32), in_=tab_scales[0].bitcast(I32).unsqueeze(1).to_broadcast([16, 8, T // 4])
+        )
+        nc.sync.dma_start(
+            out=w2s_raw[:].bitcast(I32), in_=w2_scales[0].bitcast(I32).unsqueeze(1).to_broadcast([16, 8, H // 4])
+        )
+
+        def load_weight(w, b, tag):
+            raw = keep.tile([P, 4, BANK], F32, name="raw_%s%d" % (tag, b), tag=tag, align_bytes=64)
+            nc.sync.dma_start(out=raw[:], in_=w[:, b * BANK : (b + 1) * BANK].rearrange("(p j) c -> p j c", j=4))
+            return raw
+
+        w1_raw = [load_weight(w1, 0, "w1raw")]
+        w2_raw = keep.tile([P, 2 * H], U8, name="w2_raw", tag="w2raw", align_bytes=64)
+        nc.sync.dma_start(out=w2_raw[:].bitcast(I32), in_=w2_words[0].bitcast(I32))
+        tabw = keep.tile([P, T], I32, name="tabw", tag="tabw", align_bytes=64)
+        nc.sync.dma_start(out=tabw[:], in_=tab_words[0].rearrange("p t i -> p (t i)").bitcast(I32))
+
+        nc.sync.dma_start(pos1_t[:], pos1)
+        nc.sync.dma_start(pos2_t[:], pos2)
+        planes = keep.tile([P, S + H], U8, name="planes", align_bytes=64)
+        picked_scales = keep.tile([P, S], U8, name="picked_scales", tag="w3raw", align_bytes=64)
+        nc.vector.tensor_copy(picked_scales[:], tabs[:].indirect(offs_t[:]))
+        nc.vector.tensor_copy(
+            out=planes[:, S:].rearrange("p (b t m) -> p b t m", b=2, t=4),
+            in_=w2s_raw[:].rearrange("p (b m t) -> p b t m", b=2, t=4),
+        )
+        nc.vector.tensor_copy(out=planes[:, :S].bitcast(I32), in_=picked_scales[:].bitcast(I32))
+        for r in range(1, 4):
+            nc.sync.dma_start(
+                out=planes[:].bitcast(I32)[r:P:32, :], in_=planes[:].bitcast(I32)[8 * r : P : 32, :]
+            )
+        w3_raw = [load_weight(w3, 0, "w3raw")]
+
+        def interleave(raw, pair, name, engine):
+            grouped = keep.tile([P, 2, P, 4], BF16, name="g_" + name, tag="g_" + name, align_bytes=64)
+            src = raw[:].rearrange("p j (m t) -> p m j t", t=4)[:, :, :, 2 * pair : 2 * pair + 2]
+            dst = grouped[:].rearrange("p t m j -> p m j t")
+            if engine == "scalar":
+                nc.scalar.copy(out=dst, in_=src)
+            else:
+                nc.vector.tensor_copy(out=dst, in_=src)
+            return grouped
+
+        def quantize(grouped, width, name):
+            codes = keep.tile([P, width], U32, name="c_" + name, align_bytes=64)
+            scales = keep.tile([P, width], U8, name="s_" + name, align_bytes=64)
+            nc.vector.quantize_mx(out=codes[:].bitcast(FP8X4), scales=scales[:], in_=grouped)
+            return codes, scales
+
+        def quantize_weight(grouped, name):
+            return quantize(grouped[:].rearrange("p t m j -> p (t m j)"), 2 * P, name)
+
+        g1 = {}
+        g3 = {}
+        q1 = {}
+        q3 = {}
+        g1[0] = interleave(w1_raw[0], 0, "w1_0", "scalar")
+        w2p = keep.tile([P, 2 * H], U8, name="w2p", align_bytes=64)
+        nc.vector.tensor_copy(
+            out=w2p[:].bitcast(U16).rearrange("p (b t m) -> p b t m", b=2, t=4),
+            in_=w2_raw[:].bitcast(U16).rearrange("p (b m t) -> p b t m", b=2, t=4),
+        )
+        q1[0] = quantize_weight(g1[0], "w1_0")
+        g1[1] = interleave(w1_raw[0], 1, "w1_1", "scalar")
+
+        vt = keep.tile([P, S], U32, name="vt", tag="tabs", align_bytes=64)
+        v = [vt[:, :BANK], vt[:, BANK:]]
+        for s in range(2):
+            nc.vector.tensor_copy(v[s], tabw[:].bitcast(U32).indirect(offs_t[:, 32 * s : 32 * (s + 1)]))
+        w1_raw.append(load_weight(w1, 1, "tabw"))
+        g3[0] = interleave(w3_raw[0], 0, "w3_0", "vector")
+        q3[0] = quantize_weight(g3[0], "w3_0")
+
+        w4_plane = keep.tile([P, 2, N], U8, name="w4_plane", tag="g_w3_0", align_bytes=64)
+        nc.vector.memset(w4_plane[:].rearrange("p a n -> p (a n)").bitcast(I32), 0)
+        for d in range(4):
+            nc.sync.dma_start(
+                out=w4_plane[:].bitcast(I32)[32 * d : 32 * d + 4, :, :],
+                in_=w4_scales[:, 4 * d : 4 * d + 4, :].rearrange("a q n -> q a n").bitcast(I32),
+            )
+        w4 = keep.tile([P, 2, N], I32, name="w4", tag="g_w1_1", align_bytes=64)
+        nc.sync.dma_start(out=w4[:], in_=w4_words.rearrange("a p n i -> p a (n i)").bitcast(I32))
+
+        slots = keep.tile([P, 9, S], F32, name="slots", align_bytes=64)
+        hs = {}
+        leads = {}
+
+        def first_stage(u):
+            pair, e = divmod(u, 2)
+            h = ring.tile([P, S], F32, name="h", bufs=5)
+            hs[u] = h
+            cs = []
+            for s in range(2):
+                vs = planes[:, BANK * s : BANK * (s + 1)]
+                a_ps = psum.tile([P, BANK], F32, name="a_ps", tag="a", bufs=2)
+                b_ps = psum.tile([P, BANK], F32, name="b_ps", tag="b", bufs=3)
+                c_ps = psum.tile([P, BANK], F32, name="c_ps", tag="c", bufs=3)
+                cols = slice(P * e, P * (e + 1))
+                nc.tensor.matmul_mx(
+                    out=a_ps[:], lhsT=q1[pair][0][:, cols].bitcast(FP8X4), lhsT_scale=q1[pair][1][:, cols],
+                    rhs=v[s].bitcast(FP8X4), rhs_scale=vs, start=True, stop=True,
+                )
+                nc.tensor.matmul_mx(
+                    out=b_ps[:], lhsT=w2p[:, 2 * P * u : 2 * P * (u + 1)].bitcast(FP4X4),
+                    lhsT_scale=planes[:, S + P * u : S + P * (u + 1)],
+                    rhs=v[s].bitcast(FP8X4), rhs_scale=vs, start=True, stop=True,
+                )
+                nc.tensor.matmul_mx(
+                    out=c_ps[:], lhsT=q3[pair][0][:, cols].bitcast(FP8X4), lhsT_scale=q3[pair][1][:, cols],
+                    rhs=v[s].bitcast(FP8X4), rhs_scale=vs, start=True, stop=True,
+                )
+                a_sb = ring.tile([P, BANK], F32, name="a_sb")
+                nc.scalar.copy(out=a_sb[:], in_=a_ps[:])
+                nc.vector.tensor_tensor(slots[:, u, BANK * s : BANK * (s + 1)], a_sb[:], b_ps[:], ALU.max)
+                cs.append(c_ps)
+            for s in range(2):
+                half = slice(BANK * s, BANK * (s + 1))
+                nc.vector.tensor_tensor(h[:, half], slots[:, u, half], cs[s][:], ALU.mult)
+
+        def pick_lead(u, c0, c1, dst):
+            nc.vector.tensor_copy(dst, hs[u][:].indirect(pos1_t[:, c0 // 16 : c1 // 16]))
+            nc.scalar.activation(dst, dst, ACT.Abs)
+            leads[u, c0] = dst
+
+        def pick_trail(u, c0, c1, dst):
+            nc.vector.tensor_tensor(dst, hs[u][:].indirect(pos2_t[:, c0 // 16 : c1 // 16]), leads[u, c0], ALU.add)
+
+        def round_z(zf, width, name):
+            zb = keep.tile([P, width, 4], BF16, name="zb_" + name, align_bytes=64)
+            nc.scalar.copy(
+                out=zb[:].rearrange("p (c i) t -> p c t i", i=4), in_=zf.rearrange("p t (c i) -> p c t i", i=4)
+            )
+            return zb
+
+        def width_of(u):
+            return PK if u < 4 else HALF
+
+        qz = {}
+        for u in range(8):
+            if u == 1:
+                q1[1] = quantize_weight(g1[1], "w1_1")
+                g3[1] = interleave(w3_raw[0], 1, "w3_1", "scalar")
+                w3_raw.append(load_weight(w3, 1, "w3raw"))
+                q3[1] = quantize_weight(g3[1], "w3_1")
+            if u in (2, 3, 4, 5):
+                pair = 2 + (u - 2) // 2
+                if u % 2 == 0:
+                    g1[pair] = interleave(w1_raw[1], pair - 2, "w1_%d" % pair, "scalar")
+                else:
+                    g3[pair] = interleave(w3_raw[1], pair - 2, "w3_%d" % pair, "scalar")
+            if u in (4, 6):
+                q1[u // 2] = quantize_weight(g1[u // 2], "w1_%d" % (u // 2))
+                q3[u // 2] = quantize_weight(g3[u // 2], "w3_%d" % (u // 2))
+            first_stage(u)
+            if u > 0:
+                wd = width_of(u - 1)
+                pick_trail(u - 1, 0, wd, slots[:, u, S - wd :])
+            lead = ring.tile([P, width_of(u)], F32, name="lead", bufs=3)
+            pick_lead(u, 0, width_of(u), lead[:])
+            if u == 4:
+                zb0 = round_z(slots[:, 1:5, S - PK :], PK, "0")
+            if u == 5:
+                qz[0] = quantize(zb0[:].rearrange("p m t -> p (m t)"), PK, "z0")
+
+        z_late = keep.tile([P, 4, HALF], F32, name="z_late", align_bytes=64)
+        lead7 = ring.tile([P, HALF], F32, name="lead", bufs=3)
+        late_leads = [slots[:, 7, 2 * HALF : 3 * HALF], slots[:, 7, 0:HALF], slots[:, 7, HALF : 2 * HALF], lead7[:]]
+
+        def second_stage_open(mh):
+            banks = []
+            for j in range(2):
+                y = psum.tile([P, 2, HALF], F32, name="y_ps", tag="b" if mh == 0 else "c", bufs=3)
+                for i in range(2):
+                    second_pass(y, j, i, 0, qz[0], slice(HALF * mh, HALF * (mh + 1)), i == 0, False)
+                banks.append(y)
+            return banks
+
+        def second_pass(y, j, i, a, q, mcols, start, stop):
+            ncols = slice(P * (2 * j + i), P * (2 * j + i + 1))
+            nc.tensor.matmul_mx(
+                out=y[:, i, :], lhsT=w4[:, a, ncols].bitcast(FP8X4), lhsT_scale=w4_plane[:, a, ncols],
+                rhs=q[0][:, mcols].bitcast(FP8X4), rhs_scale=q[1][:, mcols], start=start, stop=stop,
+            )
+
+        def second_stage_close(banks, q):
+            for j in range(2):
+                for i in range(2):
+                    second_pass(banks[j], j, i, 1, q, slice(0, HALF), False, i == 1)
+
+        out_v = out.rearrange("(n p) m -> p n m", p=P)
+
+        def finish(y, j, mh, on_vector):
+            sq = ring.tile([P, 2, HALF], F32, name="sq")
+            if on_vector:
+                y_sb = ring.tile([P, 2, HALF], F32, name="y_sb", bufs=1)
+                nc.vector.tensor_copy(out=y_sb[:], in_=y[:])
+                nc.vector.tensor_tensor(sq[:], y_sb[:], y_sb[:], ALU.mult)
+            else:
+                nc.scalar.activation(sq[:], y[:], ACT.Square)
+            res = ring.tile([P, 2, HALF], F32, name="res")
+            nc.scalar.activation(res[:], sq[:], ACT.Ln, bias=1.0)
+            nc.sync.dma_start(out=out_v[:, 2 * j : 2 * j + 2, HALF * mh : HALF * (mh + 1)], in_=res[:])
+
+        y0 = second_stage_open(0)
+        y1 = second_stage_open(1)
+        pick_lead(4, HALF, PK, late_leads[0])
+        pick_trail(7, 0, HALF, slots[:, 8, S - HALF :])
+        pick_lead(5, HALF, PK, late_leads[1])
+        zb1 = round_z(slots[:, 5:9, S - HALF :], HALF, "1")
+        pick_trail(4, HALF, PK, z_late[:, 0, :])
+        pick_lead(6, HALF, PK, late_leads[2])
+        q10 = quantize(zb1[:].rearrange("p m t -> p (m t)"), HALF, "z1")
+        second_stage_close(y0, q10)
+        pick_trail(5, HALF, PK, z_late[:, 1, :])
+        pick_lead(7, HALF, PK, late_leads[3])
+        pick_trail(6, HALF, PK, z_late[:, 2, :])
+        finish(y0[0], 0, 0, False)
+        pick_trail(7, HALF, PK, z_late[:, 3, :])
+        finish(y0[1], 1, 0, False)
+        zb2 = keep.tile([P, HALF, 4], BF16, name="zb_2", align_bytes=64)
+        nc.vector.tensor_copy(
+            out=zb2[:].rearrange("p (c i) t -> p c t i", i=4), in_=z_late[:].rearrange("p t (c i) -> p c t i", i=4)
+        )
+        q11 = quantize(zb2[:].rearrange("p m t -> p (m t)"), HALF, "z2")
+        second_stage_close(y1, q11)
+        finish(y1[0], 0, 1, False)
+        finish(y1[1], 1, 1, True)

@@ -19,6 +19,9 @@ ACT = mybir.ActivationFunctionType
 P = 128
 BANK = 512
 HALF = 256
+GW = 512
+LAG = 1
+IL1 = "scalar"
 
 
 def tile_list_belt_ejector_strengths_kernel(
@@ -127,61 +130,76 @@ def tile_list_belt_ejector_strengths_kernel(
         w4 = keep.tile([P, 2, N], I32, name="w4", tag="g_w1_1", align_bytes=64)
         nc.sync.dma_start(out=w4[:], in_=w4_words.rearrange("a p n i -> p a (n i)").bitcast(I32))
 
-        slots = keep.tile([P, 9, S], F32, name="slots", align_bytes=64)
         hs = {}
         leads = {}
+        a_first = {}
+        slots = keep.tile([P, 11, BANK], F32, name="slots", align_bytes=64)
+        hs[0] = keep.tile([P, S], F32, name="h0")
 
         def first_stage(u):
             pair, e = divmod(u, 2)
-            h = ring.tile([P, S], F32, name="h", bufs=5)
-            hs[u] = h
-            cs = []
+            cols = slice(P * e, P * (e + 1))
+            on_gpsimd = GW if 0 < u < 7 else 0
+            if u < 7:
+                m = ring.tile([P, S], F32, name="m", bufs=3)
+            else:
+                m = keep.tile([P, S], F32, name="m7", tag="last", align_bytes=64)
+            c_sb = ring.tile([P, GW], F32, name="c_sb", bufs=3) if on_gpsimd else None
+            a_first[u] = keep.tile([P, BANK], F32, name="a0_%d" % u, tag="ah%d" % u)
+            later = []
             for s in range(2):
-                vs = planes[:, BANK * s : BANK * (s + 1)]
+                half = slice(BANK * s, BANK * (s + 1))
                 a_ps = psum.tile([P, BANK], F32, name="a_ps", tag="a", bufs=2)
                 b_ps = psum.tile([P, BANK], F32, name="b_ps", tag="b", bufs=3)
                 c_ps = psum.tile([P, BANK], F32, name="c_ps", tag="c", bufs=3)
-                cols = slice(P * e, P * (e + 1))
                 nc.tensor.matmul_mx(
                     out=a_ps[:], lhsT=q1[pair][0][:, cols].bitcast(FP8X4), lhsT_scale=q1[pair][1][:, cols],
-                    rhs=v[s].bitcast(FP8X4), rhs_scale=vs, start=True, stop=True,
+                    rhs=v[s].bitcast(FP8X4), rhs_scale=planes[:, half], start=True, stop=True,
                 )
                 nc.tensor.matmul_mx(
                     out=b_ps[:], lhsT=w2p[:, 2 * P * u : 2 * P * (u + 1)].bitcast(FP4X4),
                     lhsT_scale=planes[:, S + P * u : S + P * (u + 1)],
-                    rhs=v[s].bitcast(FP8X4), rhs_scale=vs, start=True, stop=True,
+                    rhs=v[s].bitcast(FP8X4), rhs_scale=planes[:, half], start=True, stop=True,
                 )
                 nc.tensor.matmul_mx(
                     out=c_ps[:], lhsT=q3[pair][0][:, cols].bitcast(FP8X4), lhsT_scale=q3[pair][1][:, cols],
-                    rhs=v[s].bitcast(FP8X4), rhs_scale=vs, start=True, stop=True,
+                    rhs=v[s].bitcast(FP8X4), rhs_scale=planes[:, half], start=True, stop=True,
                 )
-                a_sb = ring.tile([P, BANK], F32, name="a_sb")
-                nc.scalar.copy(out=a_sb[:], in_=a_ps[:])
-                nc.vector.tensor_tensor(slots[:, u, BANK * s : BANK * (s + 1)], a_sb[:], b_ps[:], ALU.max)
-                cs.append(c_ps)
-            for s in range(2):
-                half = slice(BANK * s, BANK * (s + 1))
-                nc.vector.tensor_tensor(h[:, half], slots[:, u, half], cs[s][:], ALU.mult)
+                a_sb = a_first[u][:] if s == 0 else slots[:, u, :]
+                nc.scalar.copy(out=a_sb, in_=a_ps[:])
+                nc.vector.tensor_tensor(m[:, half], a_sb, b_ps[:], ALU.max)
+                later.append((half, c_ps))
+            for half, c_ps in later:
+                if half.start >= S - on_gpsimd:
+                    nc.scalar.copy(out=c_sb[:, half.start - (S - GW) : half.stop - (S - GW)], in_=c_ps[:])
+                else:
+                    nc.vector.tensor_tensor(hs[u][:, half], m[:, half], c_ps[:], ALU.mult)
+            if u < 6:
+                hs[u + 1] = keep.tile([P, S], F32, name="h%d" % (u + 1), tag="ah%d" % u)
+            elif u == 6:
+                hs[7] = keep.tile([P, S], F32, name="h7")
+            return m, c_sb
 
-        def pick_lead(u, c0, c1, dst):
-            nc.vector.tensor_copy(dst, hs[u][:].indirect(pos1_t[:, c0 // 16 : c1 // 16]))
+        def pick_lead(u, dst):
+            nc.vector.tensor_copy(dst, hs[u][:].indirect(pos1_t[:]))
             nc.scalar.activation(dst, dst, ACT.Abs)
-            leads[u, c0] = dst
+            leads[u] = dst
 
         def pick_trail(u, c0, c1, dst):
-            nc.vector.tensor_tensor(dst, hs[u][:].indirect(pos2_t[:, c0 // 16 : c1 // 16]), leads[u, c0], ALU.add)
-
-        def round_z(zf, width, name):
-            zb = keep.tile([P, width, 4], BF16, name="zb_" + name, align_bytes=64)
-            nc.scalar.copy(
-                out=zb[:].rearrange("p (c i) t -> p c t i", i=4), in_=zf.rearrange("p t (c i) -> p c t i", i=4)
+            nc.vector.tensor_tensor(
+                dst, hs[u][:].indirect(pos2_t[:, c0 // 16 : c1 // 16]), leads[u][:, c0:c1], ALU.add
             )
-            return zb
 
-        def width_of(u):
-            return PK if u < 4 else HALF
+        def round_z(engine_copy, zf, zb):
+            engine_copy(
+                out=zb.rearrange("p (c i t) -> p c t i", i=4, t=4), in_=zf.rearrange("p t (c i) -> p c t i", i=4)
+            )
 
-        qz = {}
+        def early_trail(u):
+            wd = PK if u < 5 else HALF
+            pick_trail(u, 0, wd, slots[:, u + LAG + 1, :wd])
+
+        zb0 = keep.tile([P, 4 * PK], BF16, name="zb0", align_bytes=64)
         for u in range(8):
             if u == 1:
                 q1[1] = quantize_weight(g1[1], "w1_1")
@@ -191,35 +209,28 @@ def tile_list_belt_ejector_strengths_kernel(
             if u in (2, 3, 4, 5):
                 pair = 2 + (u - 2) // 2
                 if u % 2 == 0:
-                    g1[pair] = interleave(w1_raw[1], pair - 2, "w1_%d" % pair, "scalar")
+                    g1[pair] = interleave(w1_raw[1], pair - 2, "w1_%d" % pair, IL1)
                 else:
                     g3[pair] = interleave(w3_raw[1], pair - 2, "w3_%d" % pair, "scalar")
             if u in (4, 6):
                 q1[u // 2] = quantize_weight(g1[u // 2], "w1_%d" % (u // 2))
                 q3[u // 2] = quantize_weight(g3[u // 2], "w3_%d" % (u // 2))
-            first_stage(u)
-            if u > 0:
-                wd = width_of(u - 1)
-                pick_trail(u - 1, 0, wd, slots[:, u, S - wd :])
-            lead = ring.tile([P, width_of(u)], F32, name="lead", bufs=3)
-            pick_lead(u, 0, width_of(u), lead[:])
-            if u == 4:
-                zb0 = round_z(slots[:, 1:5, S - PK :], PK, "0")
-            if u == 5:
-                qz[0] = quantize(zb0[:].rearrange("p m t -> p (m t)"), PK, "z0")
-
-        z_late = keep.tile([P, 4, HALF], F32, name="z_late", align_bytes=64)
-        lead7 = ring.tile([P, HALF], F32, name="lead", bufs=3)
-        late_leads = [slots[:, 7, 2 * HALF : 3 * HALF], slots[:, 7, 0:HALF], slots[:, 7, HALF : 2 * HALF], lead7[:]]
-
-        def second_stage_open(mh):
-            banks = []
-            for j in range(2):
-                y = psum.tile([P, 2, HALF], F32, name="y_ps", tag="b" if mh == 0 else "c", bufs=3)
-                for i in range(2):
-                    second_pass(y, j, i, 0, qz[0], slice(HALF * mh, HALF * (mh + 1)), i == 0, False)
-                banks.append(y)
-            return banks
+            m, c_sb = first_stage(u)
+            if u == 7:
+                last = keep.tile([P, 2, PK], F32, name="last", tag="last", align_bytes=64)
+            if u >= LAG:
+                if u - LAG == 6:
+                    home = last[:, 0, :]
+                else:
+                    home = hs[u + 1][:, S - PK :] if u < 6 else a_first[u][:]
+                pick_lead(u - LAG, home)
+            if u > LAG:
+                early_trail(u - LAG - 1)
+            if c_sb is not None:
+                nc.gpsimd.tensor_tensor(hs[u][:, S - GW :], m[:, S - GW :], c_sb[:], ALU.mult)
+            if u == 4 + LAG:
+                round_z(nc.scalar.copy, slots[:, LAG + 1 : LAG + 5, :], zb0[:])
+        qz0 = quantize(zb0[:], PK, "z0")
 
         def second_pass(y, j, i, a, q, mcols, start, stop):
             ncols = slice(P * (2 * j + i), P * (2 * j + i + 1))
@@ -228,46 +239,52 @@ def tile_list_belt_ejector_strengths_kernel(
                 rhs=q[0][:, mcols].bitcast(FP8X4), rhs_scale=q[1][:, mcols], start=start, stop=stop,
             )
 
-        def second_stage_close(banks, q):
+        def second_stage_open(mh):
+            banks = []
             for j in range(2):
+                y = psum.tile([P, 2, HALF], F32, name="y_ps", tag="a", bufs=2)
                 for i in range(2):
-                    second_pass(banks[j], j, i, 1, q, slice(0, HALF), False, i == 1)
+                    second_pass(y, j, i, 0, qz0, slice(HALF * mh, HALF * (mh + 1)), i == 0, False)
+                banks.append(y)
+            return banks
 
         out_v = out.rearrange("(n p) m -> p n m", p=P)
 
-        def finish(y, j, mh, on_vector):
-            sq = ring.tile([P, 2, HALF], F32, name="sq")
-            if on_vector:
-                y_sb = ring.tile([P, 2, HALF], F32, name="y_sb", bufs=1)
-                nc.vector.tensor_copy(out=y_sb[:], in_=y[:])
-                nc.vector.tensor_tensor(sq[:], y_sb[:], y_sb[:], ALU.mult)
-            else:
-                nc.scalar.activation(sq[:], y[:], ACT.Square)
-            res = ring.tile([P, 2, HALF], F32, name="res")
-            nc.scalar.activation(res[:], sq[:], ACT.Ln, bias=1.0)
-            nc.sync.dma_start(out=out_v[:, 2 * j : 2 * j + 2, HALF * mh : HALF * (mh + 1)], in_=res[:])
+        def second_stage_close(banks, q, mh):
+            squares = []
+            for j in range(2):
+                for i in range(2):
+                    second_pass(banks[j], j, i, 1, q, slice(0, HALF), False, i == 1)
+                sq = ring.tile([P, 2, HALF], F32, name="sq")
+                nc.scalar.activation(sq[:], banks[j][:], ACT.Square)
+                squares.append(sq)
+            for j in range(2):
+                res = ring.tile([P, 2, HALF], F32, name="res")
+                nc.scalar.activation(res[:], squares[j][:], ACT.Ln, bias=1.0)
+                nc.sync.dma_start(out=out_v[:, 2 * j : 2 * j + 2, HALF * mh : HALF * (mh + 1)], in_=res[:])
 
         y0 = second_stage_open(0)
-        y1 = second_stage_open(1)
-        pick_lead(4, HALF, PK, late_leads[0])
-        pick_trail(7, 0, HALF, slots[:, 8, S - HALF :])
-        pick_lead(5, HALF, PK, late_leads[1])
-        zb1 = round_z(slots[:, 5:9, S - HALF :], HALF, "1")
-        pick_trail(4, HALF, PK, z_late[:, 0, :])
-        pick_lead(6, HALF, PK, late_leads[2])
-        q10 = quantize(zb1[:].rearrange("p m t -> p (m t)"), HALF, "z1")
-        second_stage_close(y0, q10)
+        z_late = slots[:, LAG + 5 : LAG + 9, HALF:]
+        zb1 = z_late[:, 2:4, :].bitcast(BF16)
+        pick_lead(7, last[:, 1, :])
+        early_trail(6)
+        early_trail(7)
         pick_trail(5, HALF, PK, z_late[:, 1, :])
-        pick_lead(7, HALF, PK, late_leads[3])
-        pick_trail(6, HALF, PK, z_late[:, 2, :])
-        finish(y0[0], 0, 0, False)
-        pick_trail(7, HALF, PK, z_late[:, 3, :])
-        finish(y0[1], 1, 0, False)
-        zb2 = keep.tile([P, HALF, 4], BF16, name="zb_2", align_bytes=64)
         nc.vector.tensor_copy(
-            out=zb2[:].rearrange("p (c i) t -> p c t i", i=4), in_=z_late[:].rearrange("p t (c i) -> p c t i", i=4)
+            out=zb1.rearrange("p g (c i t) -> p g c t i", i=4, t=4),
+            in_=slots[:, LAG + 5 : LAG + 9, :HALF].rearrange("p t (g c i) -> p g c t i", g=2, i=4),
         )
-        q11 = quantize(zb2[:].rearrange("p m t -> p (m t)"), HALF, "z2")
-        second_stage_close(y1, q11)
-        finish(y1[0], 0, 1, False)
-        finish(y1[1], 1, 1, True)
+        z1_codes = keep.tile([P, HALF], U32, name="z1_codes", align_bytes=64)
+        z1_scales = keep.tile([P, HALF], U8, name="z1_scales", align_bytes=64)
+        for g in range(2):
+            cols = slice(P * g, P * (g + 1))
+            nc.vector.quantize_mx(out=z1_codes[:, cols].bitcast(FP8X4), scales=z1_scales[:, cols], in_=zb1[:, g, :])
+        qz1 = (z1_codes, z1_scales)
+        second_stage_close(y0, qz1, 0)
+        y1 = second_stage_open(1)
+        pick_trail(6, HALF, PK, z_late[:, 2, :])
+        pick_trail(7, HALF, PK, z_late[:, 3, :])
+        zb2 = keep.tile([P, 4 * HALF], BF16, name="zb2", align_bytes=64)
+        round_z(nc.vector.tensor_copy, z_late, zb2[:])
+        qz2 = quantize(zb2[:], HALF, "z2")
+        second_stage_close(y1, qz2, 1)

@@ -19,8 +19,8 @@ ACT = mybir.ActivationFunctionType
 P = 128
 BANK = 512
 HALF = 256
-GW = 512
-LAG = 1
+GW = 768
+LAG = 2
 IL1 = "scalar"
 
 
@@ -169,11 +169,17 @@ def tile_list_belt_ejector_strengths_kernel(
                 nc.scalar.copy(out=a_sb, in_=a_ps[:])
                 nc.vector.tensor_tensor(m[:, half], a_sb, b_ps[:], ALU.max)
                 later.append((half, c_ps))
+            cut = S - on_gpsimd
             for half, c_ps in later:
-                if half.start >= S - on_gpsimd:
-                    nc.scalar.copy(out=c_sb[:, half.start - (S - GW) : half.stop - (S - GW)], in_=c_ps[:])
-                else:
-                    nc.vector.tensor_tensor(hs[u][:, half], m[:, half], c_ps[:], ALU.mult)
+                lo = max(half.start, cut)
+                if lo < half.stop:
+                    nc.scalar.copy(out=c_sb[:, lo - cut : half.stop - cut], in_=c_ps[:, lo - half.start :])
+            for half, c_ps in later:
+                hi = min(half.stop, cut)
+                if hi > half.start:
+                    nc.vector.tensor_tensor(
+                        hs[u][:, half.start : hi], m[:, half.start : hi], c_ps[:, : hi - half.start], ALU.mult
+                    )
             if u < 6:
                 hs[u + 1] = keep.tile([P, S], F32, name="h%d" % (u + 1), tag="ah%d" % u)
             elif u == 6:
@@ -266,7 +272,9 @@ def tile_list_belt_ejector_strengths_kernel(
         y0 = second_stage_open(0)
         z_late = slots[:, LAG + 5 : LAG + 9, HALF:]
         zb1 = z_late[:, 2:4, :].bitcast(BF16)
+        pick_lead(6, last[:, 0, :])
         pick_lead(7, last[:, 1, :])
+        early_trail(5)
         early_trail(6)
         early_trail(7)
         pick_trail(5, HALF, PK, z_late[:, 1, :])

from contextlib import ExitStack

import concourse.mybir as mybir

K, T, S, PK, H, N = 512, 2048, 1024, 512, 1024, 512
FLOPS = 2 * (3 * K * H * S + H * N * PK)

F32 = mybir.dt.float32
BF16 = mybir.dt.bfloat16
I32 = mybir.dt.int32
U32 = mybir.dt.uint32
U16 = mybir.dt.uint16
U8 = mybir.dt.uint8
FP8X4 = mybir.dt.float8_e4m3fn_x4
FP4X4 = mybir.dt.float4_e2m1fn_x4
ALU = mybir.AluOpType
ACT = mybir.ActivationFunctionType

P = 128
BANK = 512
HALF = 256
GW = 768
LAG = 2
IL1 = "scalar"


def tile_list_belt_ejector_strengths_kernel(
    tc, tab_words, tab_scales, offs, pos1, pos2, w1, w2_words, w2_scales, w3, w4_words, w4_scales, out
):
    nc = tc.nc
    with ExitStack() as ctx:
        lists = ctx.enter_context(tc.tile_pool(name="lists", bufs=1))
        keep = ctx.enter_context(tc.tile_pool(name="keep", bufs=1))
        ring = ctx.enter_context(tc.tile_pool(name="ring", bufs=4))
        psum = ctx.enter_context(tc.psum_pool(name="psum", bufs=1))

        offs_t = lists.tile([P, S // 16], U16, name="offs_t")
        pos1_t = lists.tile([P, PK // 16], U16, name="pos1_t")
        pos2_t = lists.tile([P, PK // 16], U16, name="pos2_t")

        w2s_raw = keep.tile([P, H], U8, name="w2s_raw", align_bytes=64)
        tabs = keep.tile([P, T], U8, name="tabs", tag="tabs", align_bytes=64)

        warm = keep.tile([P, 8], F32, name="warm")
        nc.gpsimd.memset(warm[:], 1.0)
        nc.scalar.activation(warm[:, 0:1], warm[:, 4:5], ACT.Ln)

        nc.sync.dma_start(offs_t[:], offs)
        nc.sync.dma_start(
            out=tabs[:].bitcast(I32), in_=tab_scales[0].bitcast(I32).unsqueeze(1).to_broadcast([16, 8, T // 4])
        )
        nc.sync.dma_start(
            out=w2s_raw[:].bitcast(I32), in_=w2_scales[0].bitcast(I32).unsqueeze(1).to_broadcast([16, 8, H // 4])
        )

        def load_weight(w, b, tag):
            raw = keep.tile([P, 4, BANK], F32, name="raw_%s%d" % (tag, b), tag=tag, align_bytes=64)
            nc.sync.dma_start(out=raw[:], in_=w[:, b * BANK : (b + 1) * BANK].rearrange("(p j) c -> p j c", j=4))
            return raw

        w1_raw = [load_weight(w1, 0, "w1raw")]
        w2_raw = keep.tile([P, 2 * H], U8, name="w2_raw", tag="w2raw", align_bytes=64)
        nc.sync.dma_start(out=w2_raw[:].bitcast(I32), in_=w2_words[0].bitcast(I32))
        tabw = keep.tile([P, T], I32, name="tabw", tag="tabw", align_bytes=64)
        nc.sync.dma_start(out=tabw[:], in_=tab_words[0].rearrange("p t i -> p (t i)").bitcast(I32))

        nc.sync.dma_start(pos1_t[:], pos1)
        nc.sync.dma_start(pos2_t[:], pos2)
        planes = keep.tile([P, S + H], U8, name="planes", align_bytes=64)
        picked_scales = keep.tile([P, S], U8, name="picked_scales", tag="w3raw", align_bytes=64)
        nc.vector.tensor_copy(picked_scales[:], tabs[:].indirect(offs_t[:]))
        nc.vector.tensor_copy(
            out=planes[:, S:].rearrange("p (b t m) -> p b t m", b=2, t=4),
            in_=w2s_raw[:].rearrange("p (b m t) -> p b t m", b=2, t=4),
        )
        nc.vector.tensor_copy(out=planes[:, :S].bitcast(I32), in_=picked_scales[:].bitcast(I32))
        for r in range(1, 4):
            nc.sync.dma_start(
                out=planes[:].bitcast(I32)[r:P:32, :], in_=planes[:].bitcast(I32)[8 * r : P : 32, :]
            )
        w3_raw = [load_weight(w3, 0, "w3raw")]

        def interleave(raw, pair, name, engine):
            grouped = keep.tile([P, 2, P, 4], BF16, name="g_" + name, tag="g_" + name, align_bytes=64)
            src = raw[:].rearrange("p j (m t) -> p m j t", t=4)[:, :, :, 2 * pair : 2 * pair + 2]
            dst = grouped[:].rearrange("p t m j -> p m j t")
            if engine == "scalar":
                nc.scalar.copy(out=dst, in_=src)
            else:
                nc.vector.tensor_copy(out=dst, in_=src)
            return grouped

        def quantize(grouped, width, name):
            codes = keep.tile([P, width], U32, name="c_" + name, align_bytes=64)
            scales = keep.tile([P, width], U8, name="s_" + name, align_bytes=64)
            nc.vector.quantize_mx(out=codes[:].bitcast(FP8X4), scales=scales[:], in_=grouped)
            return codes, scales

        def quantize_weight(grouped, name):
            return quantize(grouped[:].rearrange("p t m j -> p (t m j)"), 2 * P, name)

        g1 = {}
        g3 = {}
        q1 = {}
        q3 = {}
        g1[0] = interleave(w1_raw[0], 0, "w1_0", "scalar")
        w2p = keep.tile([P, 2 * H], U8, name="w2p", align_bytes=64)
        nc.vector.tensor_copy(
            out=w2p[:].bitcast(U16).rearrange("p (b t m) -> p b t m", b=2, t=4),
            in_=w2_raw[:].bitcast(U16).rearrange("p (b m t) -> p b t m", b=2, t=4),
        )
        q1[0] = quantize_weight(g1[0], "w1_0")
        g1[1] = interleave(w1_raw[0], 1, "w1_1", "scalar")

        vt = keep.tile([P, S], U32, name="vt", tag="tabs", align_bytes=64)
        v = [vt[:, :BANK], vt[:, BANK:]]
        for s in range(2):
            nc.vector.tensor_copy(v[s], tabw[:].bitcast(U32).indirect(offs_t[:, 32 * s : 32 * (s + 1)]))
        w1_raw.append(load_weight(w1, 1, "tabw"))
        g3[0] = interleave(w3_raw[0], 0, "w3_0", "vector")
        q3[0] = quantize_weight(g3[0], "w3_0")

        w4_plane = keep.tile([P, 2, N], U8, name="w4_plane", tag="g_w3_0", align_bytes=64)
        nc.vector.memset(w4_plane[:].rearrange("p a n -> p (a n)").bitcast(I32), 0)
        for d in range(4):
            nc.sync.dma_start(
                out=w4_plane[:].bitcast(I32)[32 * d : 32 * d + 4, :, :],
                in_=w4_scales[:, 4 * d : 4 * d + 4, :].rearrange("a q n -> q a n").bitcast(I32),
            )
        w4 = keep.tile([P, 2, N], I32, name="w4", tag="g_w1_1", align_bytes=64)
        nc.sync.dma_start(out=w4[:], in_=w4_words.rearrange("a p n i -> p a (n i)").bitcast(I32))

        hs = {}
        leads = {}
        a_first = {}
        slots = keep.tile([P, 11, BANK], F32, name="slots", align_bytes=64)
        hs[0] = keep.tile([P, S], F32, name="h0")

        def first_stage(u):
            pair, e = divmod(u, 2)
            cols = slice(P * e, P * (e + 1))
            on_gpsimd = GW if 0 < u < 7 else 0
            if u < 7:
                m = ring.tile([P, S], F32, name="m", bufs=3)
            else:
                m = keep.tile([P, S], F32, name="m7", tag="last", align_bytes=64)
            c_sb = ring.tile([P, GW], F32, name="c_sb", bufs=3) if on_gpsimd else None
            a_first[u] = keep.tile([P, BANK], F32, name="a0_%d" % u, tag="ah%d" % u)
            later = []
            for s in range(2):
                half = slice(BANK * s, BANK * (s + 1))
                a_ps = psum.tile([P, BANK], F32, name="a_ps", tag="a", bufs=2)
                b_ps = psum.tile([P, BANK], F32, name="b_ps", tag="b", bufs=3)
                c_ps = psum.tile([P, BANK], F32, name="c_ps", tag="c", bufs=3)
                nc.tensor.matmul_mx(
                    out=a_ps[:], lhsT=q1[pair][0][:, cols].bitcast(FP8X4), lhsT_scale=q1[pair][1][:, cols],
                    rhs=v[s].bitcast(FP8X4), rhs_scale=planes[:, half], start=True, stop=True,
                )
                nc.tensor.matmul_mx(
                    out=b_ps[:], lhsT=w2p[:, 2 * P * u : 2 * P * (u + 1)].bitcast(FP4X4),
                    lhsT_scale=planes[:, S + P * u : S + P * (u + 1)],
                    rhs=v[s].bitcast(FP8X4), rhs_scale=planes[:, half], start=True, stop=True,
                )
                nc.tensor.matmul_mx(
                    out=c_ps[:], lhsT=q3[pair][0][:, cols].bitcast(FP8X4), lhsT_scale=q3[pair][1][:, cols],
                    rhs=v[s].bitcast(FP8X4), rhs_scale=planes[:, half], start=True, stop=True,
                )
                a_sb = a_first[u][:] if s == 0 else slots[:, u, :]
                nc.scalar.copy(out=a_sb, in_=a_ps[:])
                nc.vector.tensor_tensor(m[:, half], a_sb, b_ps[:], ALU.max)
                later.append((half, c_ps))
            cut = S - on_gpsimd
            for half, c_ps in later:
                lo = max(half.start, cut)
                if lo < half.stop:
                    nc.scalar.copy(out=c_sb[:, lo - cut : half.stop - cut], in_=c_ps[:, lo - half.start :])
            for half, c_ps in later:
                hi = min(half.stop, cut)
                if hi > half.start:
                    nc.vector.tensor_tensor(
                        hs[u][:, half.start : hi], m[:, half.start : hi], c_ps[:, : hi - half.start], ALU.mult
                    )
            if u < 6:
                hs[u + 1] = keep.tile([P, S], F32, name="h%d" % (u + 1), tag="ah%d" % u)
            elif u == 6:
                hs[7] = keep.tile([P, S], F32, name="h7")
            return m, c_sb

        def pick_lead(u, dst):
            nc.vector.tensor_copy(dst, hs[u][:].indirect(pos1_t[:]))
            nc.scalar.activation(dst, dst, ACT.Abs)
            leads[u] = dst

        def pick_trail(u, c0, c1, dst):
            nc.vector.tensor_tensor(
                dst, hs[u][:].indirect(pos2_t[:, c0 // 16 : c1 // 16]), leads[u][:, c0:c1], ALU.add
            )

        def round_z(engine_copy, zf, zb):
            engine_copy(
                out=zb.rearrange("p (c i t) -> p c t i", i=4, t=4), in_=zf.rearrange("p t (c i) -> p c t i", i=4)
            )

        def early_trail(u):
            wd = PK if u < 5 else HALF
            pick_trail(u, 0, wd, slots[:, u + LAG + 1, :wd])

        zb0 = keep.tile([P, 4 * PK], BF16, name="zb0", align_bytes=64)
        for u in range(8):
            if u == 1:
                q1[1] = quantize_weight(g1[1], "w1_1")
                g3[1] = interleave(w3_raw[0], 1, "w3_1", "scalar")
                w3_raw.append(load_weight(w3, 1, "w3raw"))
                q3[1] = quantize_weight(g3[1], "w3_1")
            if u in (2, 3, 4, 5):
                pair = 2 + (u - 2) // 2
                if u % 2 == 0:
                    g1[pair] = interleave(w1_raw[1], pair - 2, "w1_%d" % pair, IL1)
                else:
                    g3[pair] = interleave(w3_raw[1], pair - 2, "w3_%d" % pair, "scalar")
            if u in (4, 6):
                q1[u // 2] = quantize_weight(g1[u // 2], "w1_%d" % (u // 2))
                q3[u // 2] = quantize_weight(g3[u // 2], "w3_%d" % (u // 2))
            m, c_sb = first_stage(u)
            if u == 7:
                last = keep.tile([P, 2, PK], F32, name="last", tag="last", align_bytes=64)
            if u >= LAG:
                if u - LAG == 6:
                    home = last[:, 0, :]
                else:
                    home = hs[u + 1][:, S - PK :] if u < 6 else a_first[u][:]
                pick_lead(u - LAG, home)
            if u > LAG:
                early_trail(u - LAG - 1)
            if c_sb is not None:
                nc.gpsimd.tensor_tensor(hs[u][:, S - GW :], m[:, S - GW :], c_sb[:], ALU.mult)
            if u == 4 + LAG:
                round_z(nc.scalar.copy, slots[:, LAG + 1 : LAG + 5, :], zb0[:])
        qz0 = quantize(zb0[:], PK, "z0")

        def second_pass(y, j, i, a, q, mcols, start, stop):
            ncols = slice(P * (2 * j + i), P * (2 * j + i + 1))
            nc.tensor.matmul_mx(
                out=y[:, i, :], lhsT=w4[:, a, ncols].bitcast(FP8X4), lhsT_scale=w4_plane[:, a, ncols],
                rhs=q[0][:, mcols].bitcast(FP8X4), rhs_scale=q[1][:, mcols], start=start, stop=stop,
            )

        def second_stage_open(mh):
            banks = []
            for j in range(2):
                y = psum.tile([P, 2, HALF], F32, name="y_ps", tag="a", bufs=2)
                for i in range(2):
                    second_pass(y, j, i, 0, qz0, slice(HALF * mh, HALF * (mh + 1)), i == 0, False)
                banks.append(y)
            return banks

        out_v = out.rearrange("(n p) m -> p n m", p=P)

        def second_stage_close(banks, q, mh):
            squares = []
            for j in range(2):
                for i in range(2):
                    second_pass(banks[j], j, i, 1, q, slice(0, HALF), False, i == 1)
                sq = ring.tile([P, 2, HALF], F32, name="sq")
                nc.scalar.activation(sq[:], banks[j][:], ACT.Square)
                squares.append(sq)
            for j in range(2):
                res = ring.tile([P, 2, HALF], F32, name="res")
                nc.scalar.activation(res[:], squares[j][:], ACT.Ln, bias=1.0)
                nc.sync.dma_start(out=out_v[:, 2 * j : 2 * j + 2, HALF * mh : HALF * (mh + 1)], in_=res[:])

        y0 = second_stage_open(0)
        z_late = slots[:, LAG + 5 : LAG + 9, HALF:]
        zb1 = z_late[:, 2:4, :].bitcast(BF16)
        pick_lead(6, last[:, 0, :])
        pick_lead(7, last[:, 1, :])
        early_trail(5)
        early_trail(6)
        early_trail(7)
        pick_trail(5, HALF, PK, z_late[:, 1, :])
        nc.vector.tensor_copy(
            out=zb1.rearrange("p g (c i t) -> p g c t i", i=4, t=4),
            in_=slots[:, LAG + 5 : LAG + 9, :HALF].rearrange("p t (g c i) -> p g c t i", g=2, i=4),
        )
        z1_codes = keep.tile([P, HALF], U32, name="z1_codes", align_bytes=64)
        z1_scales = keep.tile([P, HALF], U8, name="z1_scales", align_bytes=64)
        for g in range(2):
            cols = slice(P * g, P * (g + 1))
            nc.vector.quantize_mx(out=z1_codes[:, cols].bitcast(FP8X4), scales=z1_scales[:, cols], in_=zb1[:, g, :])
        qz1 = (z1_codes, z1_scales)
        second_stage_close(y0, qz1, 0)
        y1 = second_stage_open(1)
        pick_trail(6, HALF, PK, z_late[:, 2, :])
        pick_trail(7, HALF, PK, z_late[:, 3, :])
        zb2 = keep.tile([P, 4 * HALF], BF16, name="zb2", align_bytes=64)
        round_z(nc.vector.tensor_copy, z_late, zb2[:])
        qz2 = quantize(zb2[:], HALF, "z2")
        second_stage_close(y1, qz2, 1)
